import numpy as np, ml_dtypes
CORES = [14,30,46,142,158,174,270,286,302,398,414,430]
N = 12
QP = 256
def setup_inputs(rng):
    return {"q": rng.standard_normal((N, 128, QP), dtype=np.float32).astype(ml_dtypes.bfloat16), "k": rng.standard_normal((N, 128, 128), dtype=np.float32).astype(ml_dtypes.bfloat16), "v": rng.standard_normal((N, 128, 128), dtype=np.float32).astype(ml_dtypes.bfloat16)}
def setup_inputs_big(rng):
    d = setup_inputs(rng)
    for k in ("q", "k", "v"): d[k] = (d[k].astype(np.float32) * 1024.0).astype(d[k].dtype)
    return d
def setup_inputs_small(rng):
    d = setup_inputs(rng)
    for k in ("q", "k", "v"): d[k] = (d[k].astype(np.float32) * (1 / 1024.0)).astype(d[k].dtype)
    return d
def setup_inputs_apart(rng):
    d = setup_inputs(rng)
    f = (10.0 ** rng.permutation(np.linspace(-1.5, 1.5, N))).astype(np.float32).reshape(N, 1, 1)
    for k in ("q", "k", "v"): d[k] = (d[k].astype(np.float32) * f).astype(d[k].dtype)
    return d
def reference(q, k, v):
    Q, K, V = q.astype(np.float64), k.astype(np.float64), v.astype(np.float64)
    y = np.zeros((N, 128, QP))
    for r in range(N):
        S = [K[j].T @ Q[r] for j in range(N)]
        m = np.max([s.max(axis=0) for s in S], axis=0)
        y[r] = sum(V[j].T @ np.maximum(S[j] - 0.5 * m, 0.0) for j in range(N))
    return {"y": y.astype(ml_dtypes.bfloat16)}

@@ -1,0 +1,213 @@
+from concourse.bass import DstId, RemoteDMATransfer
+from concourse.mybir import AluOpType
+
+N = 12
+SCRATCH = {
+    "qs": ("sbuf", [128, 256], "bfloat16"),
+    "KA": ("sbuf", [128, N * 128], "bfloat16"),
+    "VA": ("sbuf", [128, N * 128], "bfloat16"),
+    "RMa": ("sbuf", [128, 2, 128], "bfloat16"),
+    "RMb": ("sbuf", [128, 2, 128], "bfloat16"),
+    "TR": ("sbuf", [128, 2, 128], "bfloat16"),
+    "mc": ("sbuf", [128, 2], "bfloat16"),
+    "Z": ("sbuf", [128, 129], "bfloat16"),
+    "dz": ("dram", [129, 128], "bfloat16"),
+    "hI": ("sbuf", [128, 128], "bfloat16"),
+    "sel0": ("sbuf", [128, 128], "bfloat16"),
+    "sel1": ("sbuf", [128, 128], "bfloat16"),
+    "hrow": ("sbuf", [128, 128], "bfloat16"),
+    "ZT": ("sbuf", [128, 512], "bfloat16"),
+    "PB": ("sbuf", [128, N * 256], "bfloat16"),
+    "yo": ("sbuf", [128, 256], "bfloat16"),
+    "SB0": ("psum", [128, 512], "float32"),
+    "SB1": ("psum", [128, 512], "float32"),
+    "SB2": ("psum", [128, 512], "float32"),
+    "SB3": ("psum", [128, 512], "float32"),
+    "SB4": ("psum", [128, 512], "float32"),
+    "SB5": ("psum", [128, 512], "float32"),
+    "STa": ("psum", [128, 2, 256], "float32"),
+    "STb": ("psum", [128, 2, 256], "float32"),
+}
+SEMAPHORES = (["k%d" % j for j in range(N)] + ["v%d" % j for j in range(N)] +
+              ["qld", "snt", "cst", "d1", "d2", "sz", "std", "vmx", "sdn", "tr", "hr", "hc", "bc", "rl", "yd", "yc", "sto"])
+
+_PLAN = {}
+
+
+def _plan(T, topo):
+    if "p" in _PLAN:
+        return _PLAN["p"]
+    cores = list(T.cores)
+    hosts = max(topo.host(c) for c in cores) + 1
+    world = range(hosts * topo.CORES_PER_HOST)
+    cp, rackl, helper = {}, {}, {}
+    for r, c in enumerate(cores):
+        rackl[r] = [s for s, d in enumerate(cores) if topo.rack(topo.host(d)) == topo.rack(topo.host(c))]
+        cp[r] = [s for s, d in enumerate(cores) if topo.rack(topo.host(d)) != topo.rack(topo.host(c))
+                 and topo.chip(d) == topo.chip(c) and topo.may_write(c, d)][0]
+        helper[r] = [w for w in world if topo.host(w) == topo.host(c) and topo.chip(w) == topo.chip(c)
+                     and topo.die(w) != topo.die(c)][0]
+    _PLAN["p"] = (cores, cp, rackl, helper, dict((h, r) for r, h in helper.items()))
+    return _PLAN["p"]
+
+
+def _bits(m):
+    return bin(m).count("1")
+
+
+def _fan(g, T, topo, core, buf, slot, sem, dsts, local_sem):
+    mask = topo.mask(core, dsts[0])
+    for d in dsts:
+        mask &= topo.mask(core, d)
+    ap = buf[:, slot * 128:(slot + 1) * 128]
+    ids = []
+    for d in dsts:
+        rid, pid = topo.addr(d, core)
+        ids.append(DstId(rid=rid, pnc=pid))
+    g.remote_dma_fused([RemoteDMATransfer(dst_ids=ids, dma_engine_mask=mask, remote_sem=sem, srcs=[ap],
+                                          dsts=[ap for _ in dsts], alu_op=0)], local_sem=local_sem)
+    return _bits(mask)
+
+
+def rank_program(g, core, T, topo):
+    cores, cp, rackl, helper, helper_of = _plan(T, topo)
+    rank = T.rank_of(core)
+    S = T.sem
+
+    if rank is None:
+        if core not in helper_of:
+            return
+        r = helper_of[core]
+        c = cp[r]
+        L = rackl[r]
+        i0 = L.index(r)
+        peers = [cores[L[(i0 + s) % len(L)]] for s in range(1, len(L))]
+        n_on = _bits(topo.mask(cores[r], core) & ~topo.mask(cores[r], cores[c]))
+        g.wait_ge(S["v%d" % r], n_on)
+        sent = _fan(g, T, topo, core, T.VA, r, S["v%d" % r], [helper[c], cores[c]] + peers, S.snt)
+        g.wait_ge(S["v%d" % c], _bits(topo.mask(helper[c], core)))
+        sent += _fan(g, T, topo, core, T.VA, c, S["v%d" % c], peers, S.snt)
+        g.wait_ge(S.snt, sent)
+        return
+
+    r = rank
+    c = cp[r]
+    L = rackl[r]
+    i0 = L.index(r)
+    nL = len(L)
+    peers = [cores[L[(i0 + s) % nL]] for s in range(1, nL)]
+    before = [L[(i0 - s) % nL] for s in range(1, nL)]
+    order = [r, c] + before + [cp[s] for s in before]
+    early = 2 + len(before)
+    n_off = _bits(topo.mask(cores[c], core))
+    need = dict((j, n_off) for j in range(N))
+    need[r] = 16
+    tq, vq, sq, aq = g.tensor, g.vector, g.sync, g.scalar
+    SB = [T.SB0, T.SB1, T.SB2, T.SB3, T.SB4, T.SB5]
+    ST = [T.STa, T.STb]
+    RM = [T.RMa, T.RMb]
+
+    def col(j):
+        return slice(j * 128, (j + 1) * 128)
+
+    sq.dma_start(T.KA[:, col(r)], T.k[:, :]).then_inc(S["k%d" % r], 16)
+    aq.dma_start(T.VA[:, col(r)], T.v[:, :]).then_inc(S["v%d" % r], 16)
+    sq.dma_start(T.qs[:, :], T.q[:, :]).then_inc(S.qld, 16)
+
+    vq.memset(T.Z[:, 0:1], 0.5).then_inc(S.cst, 1)
+    vq.memset(T.Z[:, 1:129], 0.0).then_inc(S.cst, 1)
+    vq.memset(T.ZT[:, :], 0.0).then_inc(S.cst, 1)
+    vq.memset(T.sel0[0:2, :], 0.0).then_inc(S.cst, 1)
+    vq.memset(T.sel1[0:2, :], -1.0).then_inc(S.cst, 1)
+    vq.wait_ge(S.cst, 5)
+    vq.memset(T.sel0[0:1, :], -1.0).then_inc(S.cst, 1)
+    vq.memset(T.sel1[0:1, :], 0.0).then_inc(S.cst, 1)
+    aq.wait_ge(S.cst, 7)
+    aq.dma_start(T.dz[:, :], T.Z[:, :]).then_inc(S.d1, 16)
+    aq.wait_ge(S.d1, 16)
+    aq.dma_start(T.hI[:, :], T.dz[0:128, :]).then_inc(S.d2, 16)
+
+    g.wait_ge(S["k%d" % r], 16)
+    sent = _fan(g, T, topo, core, T.KA, r, S["k%d" % r], [cores[c]] + peers, S.snt)
+    g.wait_ge(S["v%d" % r], 16)
+    h = helper[r]
+    m_on = topo.mask(core, h) & ~topo.mask(core, cores[c])
+    rid, pid = topo.addr(h, core)
+    g.remote_dma(T.VA[:, col(r)], T.VA[:, col(r)], S["v%d" % r], S.snt, pid, rid, m_on)
+    sent += _bits(m_on)
+    g.wait_ge(S["k%d" % c], n_off)
+    sent += _fan(g, T, topo, core, T.KA, c, S["k%d" % c], peers, S.snt)
+    g.wait_ge(S.snt, sent)
+
+    tq.wait_ge(S.cst, 7)
+    for b in range(6):
+        tq.matmul(SB[b][:, :], T.ZT[0:1, 0:128], T.ZT[0:1, 0:512], start=True, stop=False).then_inc(S.sz, 1)
+    tq.wait_ge(S.sz, 6)
+    tq.wait_ge(S.qld, 16)
+
+    def s_table(i):
+        j = order[i]
+        tq.matmul(SB[i // 2][:, (i % 2) * 256:(i % 2) * 256 + 256], T.KA[:, col(j)], T.qs[:, :],
+                  start=False, stop=False).then_inc(S.sdn, 1)
+
+    for i, j in enumerate(order):
+        tq.wait_ge(S["k%d" % j], need[j])
+        if i >= 2:
+            tq.wait_ge(S.vmx, i - 1)
+        for blk in range(2):
+            tq.matmul(ST[i % 2][:, blk, 0:128], T.qs[:, col(blk)], T.KA[:, col(j)],
+                      start=True, stop=True).then_inc(S.std, 1)
+        if i < early:
+            s_table(i)
+    for i in range(early, N):
+        s_table(i)
+    tq.wait_ge(S.d2, 16)
+    tq.wait_ge(S.vmx, N)
+    tq.wait_ge(S.tr, 7)
+    tq.matmul(T.STa[0:2, 0, 0:128], T.mc[:, :], T.hI[:, :], start=True, stop=True).then_inc(S.hr, 1)
+    tq.wait_ge(S.hc, 1)
+    tq.wait_ge(S.sdn, N)
+    sel = [T.sel0, T.sel1]
+    for b in range(6):
+        for tab in range(2):
+            for blk in range(2):
+                o = tab * 256 + blk * 128
+                tq.matmul(SB[b][:, o:o + 128], sel[blk][0:2, :], T.hrow[0:2, :], start=False,
+                          stop=(tab == 1 and blk == 1)).then_inc(S.bc, 1)
+    for i, j in enumerate(order):
+        tq.wait_ge(S.rl, i // 2 + 1)
+        tq.wait_ge(S["v%d" % j], need[j])
+        mm = tq.matmul(T.STb[:, 0, :], T.VA[:, col(j)], T.PB[:, i * 256:(i + 1) * 256], start=(i == 0), stop=(i == N - 1))
+        if i == N - 1:
+            mm.then_inc(S.yd, 1)
+
+    for i in range(N):
+        vq.wait_ge(S.std, 2 * (i + 1))
+        if i == 0:
+            vq.tensor_copy(RM[1][:, :, :], ST[0][:, :, 0:128]).then_inc(S.vmx, 1)
+        else:
+            vq.wait_ge(S.vmx, i)
+            vq.tensor_tensor(RM[(i + 1) % 2][:, :, :], RM[i % 2][:, :, :], ST[i % 2][:, :, 0:128],
+                             AluOpType.max).then_inc(S.vmx, 1)
+    vq.wait_ge(S.vmx, N)
+    src = RM[N % 2]
+    vq.tensor_tensor(T.TR[:, :, 64:128], src[:, :, 0:64], src[:, :, 64:128], AluOpType.max).then_inc(S.tr, 1)
+    w, n = 32, 1
+    while w >= 2:
+        vq.wait_ge(S.tr, n)
+        vq.tensor_tensor(T.TR[:, :, w:2 * w], T.TR[:, :, 2 * w:3 * w], T.TR[:, :, 3 * w:4 * w],
+                         AluOpType.max).then_inc(S.tr, 1)
+        w, n = w // 2, n + 1
+    vq.wait_ge(S.tr, n)
+    vq.tensor_tensor(T.mc[:, :], T.TR[:, :, 2], T.TR[:, :, 3], AluOpType.max).then_inc(S.tr, 1)
+    vq.wait_ge(S.hr, 1)
+    vq.tensor_copy(T.hrow[0:2, :], T.STa[0:2, 0, 0:128]).then_inc(S.hc, 1)
+    for b in range(6):
+        vq.wait_ge(S.bc, 4 * (b + 1))
+        vq.tensor_tensor(T.PB[:, b * 512:(b + 1) * 512], SB[b][:, :], T.ZT[:, :], AluOpType.max).then_inc(S.rl, 1)
+    vq.wait_ge(S.yd, 1)
+    vq.tensor_copy(T.yo[:, :], T.STb[:, 0, :]).then_inc(S.yc, 1)
+
+    sq.wait_ge(S.yc, 1)
+    sq.dma_start(T.y[:, :], T.yo[:, :]).then_inc(S.sto, 16)
+    sq.wait_ge(S.sto, 16)

@@ -1,5 +1,5 @@
 from concourse.bass import DstId, RemoteDMATransfer
-from concourse.mybir import AluOpType
+from concourse.mybir import AluOpType, AxisListType, ActivationFunctionType
 
 N = 12
 SCRATCH = {
@@ -8,14 +8,12 @@ SCRATCH = {
     "VA": ("sbuf", [128, N * 128], "bfloat16"),
     "RMa": ("sbuf", [128, 2, 128], "bfloat16"),
     "RMb": ("sbuf", [128, 2, 128], "bfloat16"),
-    "TR": ("sbuf", [128, 2, 128], "bfloat16"),
-    "mc": ("sbuf", [128, 2], "bfloat16"),
+    "mc": ("sbuf", [128, 2], "float32"),
     "Z": ("sbuf", [128, 129], "bfloat16"),
     "dz": ("dram", [129, 128], "bfloat16"),
-    "hI": ("sbuf", [128, 128], "bfloat16"),
-    "sel0": ("sbuf", [128, 128], "bfloat16"),
-    "sel1": ("sbuf", [128, 128], "bfloat16"),
-    "hrow": ("sbuf", [128, 128], "bfloat16"),
+    "idn": ("sbuf", [128, 128], "bfloat16"),
+    "ones": ("sbuf", [128, 128], "bfloat16"),
+    "D": ("sbuf", [128, 256], "bfloat16"),
     "ZT": ("sbuf", [128, 512], "bfloat16"),
     "PB": ("sbuf", [128, N * 256], "bfloat16"),
     "yo": ("sbuf", [128, 256], "bfloat16"),
@@ -29,7 +27,7 @@ SCRATCH = {
     "STb": ("psum", [128, 2, 256], "float32"),
 }
 SEMAPHORES = (["k%d" % j for j in range(N)] + ["v%d" % j for j in range(N)] +
-              ["qld", "snt", "cst", "d1", "d2", "sz", "std", "vmx", "sdn", "tr", "hr", "hc", "bc", "rl", "yd", "yc", "sto"])
+              ["qld", "snt", "cst", "d1", "d2", "sz", "std", "vmx", "sdn", "tr", "dd", "bc", "rl", "rs", "yd", "yc", "sto"])
 
 _PLAN = {}
 
@@ -114,18 +112,14 @@ def rank_program(g, core, T, topo):
     aq.dma_start(T.VA[:, col(r)], T.v[:, :]).then_inc(S["v%d" % r], 16)
     sq.dma_start(T.qs[:, :], T.q[:, :]).then_inc(S.qld, 16)
 
-    vq.memset(T.Z[:, 0:1], 0.5).then_inc(S.cst, 1)
+    vq.memset(T.Z[:, 0:1], 1.0).then_inc(S.cst, 1)
     vq.memset(T.Z[:, 1:129], 0.0).then_inc(S.cst, 1)
     vq.memset(T.ZT[:, :], 0.0).then_inc(S.cst, 1)
-    vq.memset(T.sel0[0:2, :], 0.0).then_inc(S.cst, 1)
-    vq.memset(T.sel1[0:2, :], -1.0).then_inc(S.cst, 1)
-    vq.wait_ge(S.cst, 5)
-    vq.memset(T.sel0[0:1, :], -1.0).then_inc(S.cst, 1)
-    vq.memset(T.sel1[0:1, :], 0.0).then_inc(S.cst, 1)
-    aq.wait_ge(S.cst, 7)
+    vq.memset(T.ones[:, :], 1.0).then_inc(S.cst, 1)
+    aq.wait_ge(S.cst, 4)
     aq.dma_start(T.dz[:, :], T.Z[:, :]).then_inc(S.d1, 16)
     aq.wait_ge(S.d1, 16)
-    aq.dma_start(T.hI[:, :], T.dz[0:128, :]).then_inc(S.d2, 16)
+    aq.dma_start(T.idn[:, :], T.dz[0:128, :]).then_inc(S.d2, 16)
 
     g.wait_ge(S["k%d" % r], 16)
     sent = _fan(g, T, topo, core, T.KA, r, S["k%d" % r], [cores[c]] + peers, S.snt)
@@ -139,7 +133,7 @@ def rank_program(g, core, T, topo):
     sent += _fan(g, T, topo, core, T.KA, c, S["k%d" % c], peers, S.snt)
     g.wait_ge(S.snt, sent)
 
-    tq.wait_ge(S.cst, 7)
+    tq.wait_ge(S.cst, 4)
     for b in range(6):
         tq.matmul(SB[b][:, :], T.ZT[0:1, 0:128], T.ZT[0:1, 0:512], start=True, stop=False).then_inc(S.sz, 1)
     tq.wait_ge(S.sz, 6)
@@ -161,21 +155,16 @@ def rank_program(g, core, T, topo):
             s_table(i)
     for i in range(early, N):
         s_table(i)
-    tq.wait_ge(S.d2, 16)
     tq.wait_ge(S.vmx, N)
-    tq.wait_ge(S.tr, 7)
-    tq.matmul(T.STa[0:2, 0, 0:128], T.mc[:, :], T.hI[:, :], start=True, stop=True).then_inc(S.hr, 1)
-    tq.wait_ge(S.hc, 1)
     tq.wait_ge(S.sdn, N)
-    sel = [T.sel0, T.sel1]
+    tq.wait_ge(S.dd, 2)
     for b in range(6):
-        for tab in range(2):
-            for blk in range(2):
-                o = tab * 256 + blk * 128
-                tq.matmul(SB[b][:, o:o + 128], sel[blk][0:2, :], T.hrow[0:2, :], start=False,
-                          stop=(tab == 1 and blk == 1)).then_inc(S.bc, 1)
+        for t in range(2):
+            tq.matmul(SB[b][:, t * 256:(t + 1) * 256], T.ones[:, :], T.D[:, :], start=False,
+                      stop=(t == 1)).then_inc(S.bc, 1)
     for i, j in enumerate(order):
-        tq.wait_ge(S.rl, i // 2 + 1)
+        b = i // 2
+        tq.wait_ge(S.rl if b % 2 == 0 else S.rs, b // 2 + 1)
         tq.wait_ge(S["v%d" % j], need[j])
         mm = tq.matmul(T.STb[:, 0, :], T.VA[:, col(j)], T.PB[:, i * 256:(i + 1) * 256], start=(i == 0), stop=(i == N - 1))
         if i == N - 1:
@@ -189,24 +178,24 @@ def rank_program(g, core, T, topo):
             vq.wait_ge(S.vmx, i)
             vq.tensor_tensor(RM[(i + 1) % 2][:, :, :], RM[i % 2][:, :, :], ST[i % 2][:, :, 0:128],
                              AluOpType.max).then_inc(S.vmx, 1)
+    vq.wait_ge(S.d2, 16)
     vq.wait_ge(S.vmx, N)
     src = RM[N % 2]
-    vq.tensor_tensor(T.TR[:, :, 64:128], src[:, :, 0:64], src[:, :, 64:128], AluOpType.max).then_inc(S.tr, 1)
-    w, n = 32, 1
-    while w >= 2:
-        vq.wait_ge(S.tr, n)
-        vq.tensor_tensor(T.TR[:, :, w:2 * w], T.TR[:, :, 2 * w:3 * w], T.TR[:, :, 3 * w:4 * w],
-                         AluOpType.max).then_inc(S.tr, 1)
-        w, n = w // 2, n + 1
-    vq.wait_ge(S.tr, n)
-    vq.tensor_tensor(T.mc[:, :], T.TR[:, :, 2], T.TR[:, :, 3], AluOpType.max).then_inc(S.tr, 1)
-    vq.wait_ge(S.hr, 1)
-    vq.tensor_copy(T.hrow[0:2, :], T.STa[0:2, 0, 0:128]).then_inc(S.hc, 1)
-    for b in range(6):
-        vq.wait_ge(S.bc, 4 * (b + 1))
-        vq.tensor_tensor(T.PB[:, b * 512:(b + 1) * 512], SB[b][:, :], T.ZT[:, :], AluOpType.max).then_inc(S.rl, 1)
+    for blk in range(2):
+        vq.tensor_reduce(T.mc[:, blk:blk + 1], src[:, blk, :], AxisListType.X, AluOpType.max).then_inc(S.tr, 1)
+    vq.wait_ge(S.tr, 2)
+    for blk in range(2):
+        vq.tensor_scalar(T.D[:, col(blk)], T.idn[:, :], T.mc[:, blk:blk + 1], -0.5, AluOpType.mult,
+                         AluOpType.mult).then_inc(S.dd, 1)
+    for b in range(0, 6, 2):
+        vq.wait_ge(S.bc, 2 * (b + 1))
+        vq.tensor_scalar(T.PB[:, b * 512:(b + 1) * 512], SB[b][:, :], 0.0, None, AluOpType.max).then_inc(S.rl, 1)
     vq.wait_ge(S.yd, 1)
     vq.tensor_copy(T.yo[:, :], T.STb[:, 0, :]).then_inc(S.yc, 1)
+
+    for b in range(1, 6, 2):
+        aq.wait_ge(S.bc, 2 * (b + 1))
+        aq.activation(T.PB[:, b * 512:(b + 1) * 512], SB[b][:, :], ActivationFunctionType.Relu).then_inc(S.rs, 1)
 
     sq.wait_ge(S.yc, 1)
     sq.dma_start(T.y[:, :], T.yo[:, :]).then_inc(S.sto, 16)

from concourse.bass import DstId, RemoteDMATransfer
from concourse.mybir import AluOpType, AxisListType, ActivationFunctionType

N = 12
SCRATCH = {
    "qs": ("sbuf", [128, 256], "bfloat16"),
    "KA": ("sbuf", [128, N * 128], "bfloat16"),
    "VA": ("sbuf", [128, N * 128], "bfloat16"),
    "RMa": ("sbuf", [128, 2, 128], "bfloat16"),
    "RMb": ("sbuf", [128, 2, 128], "bfloat16"),
    "mc": ("sbuf", [128, 2], "float32"),
    "Z": ("sbuf", [128, 129], "bfloat16"),
    "dz": ("dram", [129, 128], "bfloat16"),
    "idn": ("sbuf", [128, 128], "bfloat16"),
    "ones": ("sbuf", [128, 128], "bfloat16"),
    "D": ("sbuf", [128, 256], "bfloat16"),
    "ZT": ("sbuf", [128, 512], "bfloat16"),
    "PB": ("sbuf", [128, N * 256], "bfloat16"),
    "yo": ("sbuf", [128, 256], "bfloat16"),
    "SB0": ("psum", [128, 512], "float32"),
    "SB1": ("psum", [128, 512], "float32"),
    "SB2": ("psum", [128, 512], "float32"),
    "SB3": ("psum", [128, 512], "float32"),
    "SB4": ("psum", [128, 512], "float32"),
    "SB5": ("psum", [128, 512], "float32"),
    "STa": ("psum", [128, 2, 256], "float32"),
    "STb": ("psum", [128, 2, 256], "float32"),
}
SEMAPHORES = (["k%d" % j for j in range(N)] + ["v%d" % j for j in range(N)] +
              ["qld", "snt", "cst", "d1", "d2", "sz", "std", "vmx", "sdn", "tr", "dd", "bc", "rl", "rs", "yd", "yc", "sto"])

_PLAN = {}


def _plan(T, topo):
    if "p" in _PLAN:
        return _PLAN["p"]
    cores = list(T.cores)
    hosts = max(topo.host(c) for c in cores) + 1
    world = range(hosts * topo.CORES_PER_HOST)
    cp, rackl, helper = {}, {}, {}
    for r, c in enumerate(cores):
        rackl[r] = [s for s, d in enumerate(cores) if topo.rack(topo.host(d)) == topo.rack(topo.host(c))]
        cp[r] = [s for s, d in enumerate(cores) if topo.rack(topo.host(d)) != topo.rack(topo.host(c))
                 and topo.chip(d) == topo.chip(c) and topo.may_write(c, d)][0]
        helper[r] = [w for w in world if topo.host(w) == topo.host(c) and topo.chip(w) == topo.chip(c)
                     and topo.die(w) != topo.die(c)][0]
    _PLAN["p"] = (cores, cp, rackl, helper, dict((h, r) for r, h in helper.items()))
    return _PLAN["p"]


def _bits(m):
    return bin(m).count("1")


def _fan(g, T, topo, core, buf, slot, sem, dsts, local_sem):
    mask = topo.mask(core, dsts[0])
    for d in dsts:
        mask &= topo.mask(core, d)
    ap = buf[:, slot * 128:(slot + 1) * 128]
    ids = []
    for d in dsts:
        rid, pid = topo.addr(d, core)
        ids.append(DstId(rid=rid, pnc=pid))
    g.remote_dma_fused([RemoteDMATransfer(dst_ids=ids, dma_engine_mask=mask, remote_sem=sem, srcs=[ap],
                                          dsts=[ap for _ in dsts], alu_op=0)], local_sem=local_sem)
    return _bits(mask)


def rank_program(g, core, T, topo):
    cores, cp, rackl, helper, helper_of = _plan(T, topo)
    rank = T.rank_of(core)
    S = T.sem

    if rank is None:
        if core not in helper_of:
            return
        r = helper_of[core]
        c = cp[r]
        L = rackl[r]
        i0 = L.index(r)
        peers = [cores[L[(i0 + s) % len(L)]] for s in range(1, len(L))]
        n_on = _bits(topo.mask(cores[r], core) & ~topo.mask(cores[r], cores[c]))
        g.wait_ge(S["v%d" % r], n_on)
        sent = _fan(g, T, topo, core, T.VA, r, S["v%d" % r], [helper[c], cores[c]] + peers, S.snt)
        g.wait_ge(S["v%d" % c], _bits(topo.mask(helper[c], core)))
        sent += _fan(g, T, topo, core, T.VA, c, S["v%d" % c], peers, S.snt)
        g.wait_ge(S.snt, sent)
        return

    r = rank
    c = cp[r]
    L = rackl[r]
    i0 = L.index(r)
    nL = len(L)
    peers = [cores[L[(i0 + s) % nL]] for s in range(1, nL)]
    before = [L[(i0 - s) % nL] for s in range(1, nL)]
    order = [r, c] + before + [cp[s] for s in before]
    early = 2 + len(before)
    n_off = _bits(topo.mask(cores[c], core))
    need = dict((j, n_off) for j in range(N))
    need[r] = 16
    tq, vq, sq, aq = g.tensor, g.vector, g.sync, g.scalar
    SB = [T.SB0, T.SB1, T.SB2, T.SB3, T.SB4, T.SB5]
    ST = [T.STa, T.STb]
    RM = [T.RMa, T.RMb]

    def col(j):
        return slice(j * 128, (j + 1) * 128)

    sq.dma_start(T.KA[:, col(r)], T.k[:, :]).then_inc(S["k%d" % r], 16)
    aq.dma_start(T.VA[:, col(r)], T.v[:, :]).then_inc(S["v%d" % r], 16)
    sq.dma_start(T.qs[:, :], T.q[:, :]).then_inc(S.qld, 16)

    vq.memset(T.Z[:, 0:1], 1.0).then_inc(S.cst, 1)
    vq.memset(T.Z[:, 1:129], 0.0).then_inc(S.cst, 1)
    vq.memset(T.ZT[:, :], 0.0).then_inc(S.cst, 1)
    vq.memset(T.ones[:, :], 1.0).then_inc(S.cst, 1)
    aq.wait_ge(S.cst, 4)
    aq.dma_start(T.dz[:, :], T.Z[:, :]).then_inc(S.d1, 16)
    aq.wait_ge(S.d1, 16)
    aq.dma_start(T.idn[:, :], T.dz[0:128, :]).then_inc(S.d2, 16)

    g.wait_ge(S["k%d" % r], 16)
    sent = _fan(g, T, topo, core, T.KA, r, S["k%d" % r], [cores[c]] + peers, S.snt)
    g.wait_ge(S["v%d" % r], 16)
    h = helper[r]
    m_on = topo.mask(core, h) & ~topo.mask(core, cores[c])
    rid, pid = topo.addr(h, core)
    g.remote_dma(T.VA[:, col(r)], T.VA[:, col(r)], S["v%d" % r], S.snt, pid, rid, m_on)
    sent += _bits(m_on)
    g.wait_ge(S["k%d" % c], n_off)
    sent += _fan(g, T, topo, core, T.KA, c, S["k%d" % c], peers, S.snt)
    g.wait_ge(S.snt, sent)

    tq.wait_ge(S.cst, 4)
    for b in range(6):
        tq.matmul(SB[b][:, :], T.ZT[0:1, 0:128], T.ZT[0:1, 0:512], start=True, stop=False).then_inc(S.sz, 1)
    tq.wait_ge(S.sz, 6)
    tq.wait_ge(S.qld, 16)

    def s_table(i):
        j = order[i]
        tq.matmul(SB[i // 2][:, (i % 2) * 256:(i % 2) * 256 + 256], T.KA[:, col(j)], T.qs[:, :],
                  start=False, stop=False).then_inc(S.sdn, 1)

    for i, j in enumerate(order):
        tq.wait_ge(S["k%d" % j], need[j])
        if i >= 2:
            tq.wait_ge(S.vmx, i - 1)
        for blk in range(2):
            tq.matmul(ST[i % 2][:, blk, 0:128], T.qs[:, col(blk)], T.KA[:, col(j)],
                      start=True, stop=True).then_inc(S.std, 1)
        if i < early:
            s_table(i)
    for i in range(early, N):
        s_table(i)
    tq.wait_ge(S.vmx, N)
    tq.wait_ge(S.sdn, N)
    tq.wait_ge(S.dd, 2)
    for b in range(6):
        for t in range(2):
            tq.matmul(SB[b][:, t * 256:(t + 1) * 256], T.ones[:, :], T.D[:, :], start=False,
                      stop=(t == 1)).then_inc(S.bc, 1)
    for i, j in enumerate(order):
        b = i // 2
        tq.wait_ge(S.rl if b % 2 == 0 else S.rs, b // 2 + 1)
        tq.wait_ge(S["v%d" % j], need[j])
        mm = tq.matmul(T.STb[:, 0, :], T.VA[:, col(j)], T.PB[:, i * 256:(i + 1) * 256], start=(i == 0), stop=(i == N - 1))
        if i == N - 1:
            mm.then_inc(S.yd, 1)

    for i in range(N):
        vq.wait_ge(S.std, 2 * (i + 1))
        if i == 0:
            vq.tensor_copy(RM[1][:, :, :], ST[0][:, :, 0:128]).then_inc(S.vmx, 1)
        else:
            vq.wait_ge(S.vmx, i)
            vq.tensor_tensor(RM[(i + 1) % 2][:, :, :], RM[i % 2][:, :, :], ST[i % 2][:, :, 0:128],
                             AluOpType.max).then_inc(S.vmx, 1)
    vq.wait_ge(S.d2, 16)
    vq.wait_ge(S.vmx, N)
    src = RM[N % 2]
    for blk in range(2):
        vq.tensor_reduce(T.mc[:, blk:blk + 1], src[:, blk, :], AxisListType.X, AluOpType.max).then_inc(S.tr, 1)
    vq.wait_ge(S.tr, 2)
    for blk in range(2):
        vq.tensor_scalar(T.D[:, col(blk)], T.idn[:, :], T.mc[:, blk:blk + 1], -0.5, AluOpType.mult,
                         AluOpType.mult).then_inc(S.dd, 1)
    for b in range(0, 6, 2):
        vq.wait_ge(S.bc, 2 * (b + 1))
        vq.tensor_scalar(T.PB[:, b * 512:(b + 1) * 512], SB[b][:, :], 0.0, None, AluOpType.max).then_inc(S.rl, 1)
    vq.wait_ge(S.yd, 1)
    vq.tensor_copy(T.yo[:, :], T.STb[:, 0, :]).then_inc(S.yc, 1)

    for b in range(1, 6, 2):
        aq.wait_ge(S.bc, 2 * (b + 1))
        aq.activation(T.PB[:, b * 512:(b + 1) * 512], SB[b][:, :], ActivationFunctionType.Relu).then_inc(S.rs, 1)

    sq.wait_ge(S.yc, 1)
    sq.dma_start(T.y[:, :], T.yo[:, :]).then_inc(S.sto, 16)
    sq.wait_ge(S.sto, 16)
